import numpy as np
import ml_dtypes


def mxq(x, axis, fmt="e4m3"):
    dtype, down = {"e4m3": (ml_dtypes.float8_e4m3fn, 7), "e5m2": (ml_dtypes.float8_e5m2, 14)}[fmt]
    v = np.moveaxis(np.asarray(x, np.float32).astype(ml_dtypes.bfloat16).astype(np.float64), axis, -1)
    blocks = v.reshape(v.shape[:-1] + (-1, 32))
    amax = np.abs(blocks).max(-1, keepdims=True)
    byte = np.maximum(np.where(amax > 0, np.frexp(amax)[1] - 1 + 127, 0) - down, 1)
    scale = np.exp2(byte - 127.0)
    codes = (blocks / scale).astype(np.float32).astype(dtype).astype(np.float64)
    return np.moveaxis((codes * scale).reshape(v.shape), -1, axis)


WIDE = False


def mx_kscale(k):
    if not WIDE:
        return np.ones(k)
    levels = np.array([10, -10, 5, -5, 0])
    if k % 512:
        return np.exp2(np.random.permutation(np.resize(levels, k // 32))).repeat(32)
    a = np.empty((k // 512, 16))
    for p in range(k // 512):
        a[p, :8] = np.random.permutation(np.resize(levels, 8))
        for g in range(8):
            far = levels[np.abs(levels - a[p, g]) >= 10]
            a[p, g + 8] = far[np.random.randint(len(far))]
    return np.exp2(a.ravel()).repeat(32)


def f64(x):
    return np.asarray(x).astype(np.float64)


def striped(idx):
    return np.tile(idx.reshape(-1, 16).T, (8, 1)).astype(np.uint16)


def unstriped(offs):
    return offs[:16].T.reshape(-1).astype(np.int64)


def striped8(idx):
    return np.concatenate([x.reshape(-1, 16).T for x in idx]).astype(np.uint16)


def runs(offs, k):
    lists = np.stack([offs[16 * r : 16 * r + 16].T.reshape(-1) for r in range(8)]).astype(np.int64)
    return lists[np.arange(k) % 512 // 64]


def pack_weight(w):
    k, n = w.shape
    w = f64(np.asarray(w, np.float32).astype(ml_dtypes.bfloat16)).reshape(k // 32, 32, n)
    amax = np.abs(w).max(1)
    byte = np.clip(np.where(amax > 0, np.frexp(amax)[1] - 1 + 127 - 7, 1), 1, 254)
    scaled = (w * np.exp2(127.0 - byte)[:, None, :]).reshape(k, n).astype(np.float32)
    words = np.ascontiguousarray(scaled.reshape(k // 512, 128, 4, n).transpose(0, 1, 3, 2)).astype(ml_dtypes.float8_e4m3fn).view(np.uint8)
    return words, np.ascontiguousarray(byte.astype(np.uint8).reshape(k // 512, 16, n))


def unpack_weight(words, scales):
    g, p, n, _ = words.shape
    vals = np.ascontiguousarray(words).view(ml_dtypes.float8_e4m3fn).astype(np.float64) * np.repeat(np.exp2(scales.astype(np.float64) - 127.0), 8, axis=1)[..., None]
    return vals.transpose(0, 1, 3, 2).reshape(g * 512, n)


def sigmoid(v):
    return 1.0 / (1.0 + np.exp(-np.maximum(v, -700.0)))


K, T, S, N, G, H, W = 512, 2048, 512, 512, 2048, 512, 256


def setup_inputs():
    n = np.random.standard_normal
    s = mx_kscale(K)[:, None]
    u = mx_kscale(S)
    packed_xT = pack_weight(n((K, T)) * s)
    packed_dT = pack_weight(n((K, G)) / s)
    perm = np.stack([np.random.permutation(S) for _ in range(8)])
    return {
        "x_words": packed_xT[0],
        "x_scales": packed_xT[1],
        "d_words": packed_dT[0],
        "d_scales": packed_dT[1],
        "gn": (np.random.uniform(0.5, 1.5, (H, 1)) * u[:, None]).astype(np.float32),
        "w1": (n((H, N)) / np.sqrt(2 * H) / u[:, None]).astype(np.float32),
        "w2": (n((K, N)) / np.sqrt(2 * K) / s).astype(np.float32),
        "sl": np.random.uniform(1.0, 2.0, (N, 1)).astype(np.float32),
        "th": (0.5 * n((N, 1))).astype(np.float32),
        "offs": striped(np.random.permutation(T)[:S]),
        "k1": striped8(np.random.randint(0, G, (8, H))),
        "n1": striped8(perm[:, :W]),
        "n2": striped8(perm[:, W:]),
        "two": striped(np.random.permutation(T)[:S]),
        "n3": striped8(np.stack([np.random.permutation(S) for _ in range(8)])),
        "n4": striped8(np.stack([np.random.permutation(S) for _ in range(8)])),
    }


def reference(x_words, x_scales, d_words, d_scales, gn, w1, w2, sl, th, offs, k1, n1, n2, two, n3, n4):
    d_k1 = unpack_weight(d_words, d_scales)[np.arange(K)[:, None], runs(k1, K)]
    xq = unpack_weight(x_words, x_scales)[:, unstriped(offs)]
    s = 0.0625 * (d_k1.T @ xq)
    pa = s[np.arange(H)[:, None], runs(n1, H)]
    pb = s[np.arange(H)[:, None], runs(n2, H)]
    ra = np.maximum(pa, pb)
    ds = s.copy()
    ds[np.arange(H)[:, None], runs(n1, H)] = ra
    z = f64(gn) * ds
    x_two = unpack_weight(x_words, x_scales)[:, unstriped(two)]
    h = mxq(f64(w1), 0, "e4m3").T @ mxq(z, 0, "e4m3") + mxq(f64(w2), 0, "e4m3").T @ x_two
    st = np.maximum(h, h[np.arange(N)[:, None], runs(n3, N)])
    sg = sigmoid(f64(sl) * (st[np.arange(N)[:, None], runs(n4, N)] - f64(th)))
    return st * sg

@@ -1,0 +1,225 @@
+from contextlib import ExitStack
+
+import concourse.mybir as mybir
+
+K, T, S, N, G, H, W = 512, 2048, 512, 512, 2048, 512, 256
+FLOPS = 2 * K * H * S + 2 * H * N * S + 2 * K * N * S
+
+F32 = mybir.dt.float32
+BF16 = mybir.dt.bfloat16
+I32 = mybir.dt.int32
+U32 = mybir.dt.uint32
+U16 = mybir.dt.uint16
+U8 = mybir.dt.uint8
+FP8X4 = mybir.dt.float8_e4m3fn_x4
+ALU = mybir.AluOpType
+ACT = mybir.ActivationFunctionType
+
+P = 128
+PACK = 4
+
+
+def tile_picked_kmixfillehh_none_p_kernel(
+    tc, x_words, x_scales, d_words, d_scales, gn, w1, w2, sl, th, offs, k1, n1, n2, two, n3, n4, out
+):
+    nc = tc.nc
+    with ExitStack() as ctx:
+        lists = ctx.enter_context(tc.tile_pool(name="lists", bufs=1))
+        keep = ctx.enter_context(tc.tile_pool(name="keep", bufs=1))
+        psum = ctx.enter_context(tc.psum_pool(name="psum", bufs=1))
+
+        def load_list(src, name):
+            held = lists.tile(list(src.shape), U16, name=name)
+            nc.sync.dma_start(held[:], src)
+            return held
+
+        d_bytes = keep.tile([P, G], U8, name="d_bytes")
+        x_bytes = keep.tile([P, T], U8, name="x_bytes")
+        for table in (d_bytes, x_bytes):
+            nc.vector.memset(table[:, : T // 2].bitcast(I32), 0)
+            nc.gpsimd.memset(table[:, T // 2 :].bitcast(I32), 0)
+
+        k1_l = load_list(k1, "k1_l")
+        d_rows = d_scales[0].rearrange("(g e) c -> e g c", e=2)
+        for e in range(2):
+            nc.sync.dma_start(d_bytes[e:P:16, :].bitcast(I32), d_rows[e].bitcast(I32))
+        offs_l = load_list(offs, "offs_l")
+        two_l = load_list(two, "two_l")
+        d_tab = keep.tile([P, G], U32, name="d_tab", tag="slot_b")
+        nc.sync.dma_start(d_tab[:].bitcast(I32), d_words[0].rearrange("p n t -> p (n t)").bitcast(I32))
+        for q in range(4):
+            nc.sync.dma_start(x_bytes[32 * q : 32 * q + 4, :].bitcast(I32), x_scales[0, 4 * q : 4 * q + 4, :].bitcast(I32))
+        x_tab = keep.tile([P, T], U32, name="x_tab", tag="slot_c", align_bytes=64)
+        nc.sync.dma_start(x_tab[:].bitcast(I32), x_words[0].rearrange("p n t -> p (n t)").bitcast(I32))
+        half_n = N // 2
+        w1_rows = w1.rearrange("(p j) c -> p j c", j=PACK)
+        w1_lo = keep.tile([P, PACK, half_n], F32, name="w1_lo")
+        nc.sync.dma_start(w1_lo[:], w1_rows[:, :, :half_n])
+        n1_l = load_list(n1, "n1_l")
+        n2_l = load_list(n2, "n2_l")
+        n3_l = load_list(n3, "n3_l")
+        n4_l = load_list(n4, "n4_l")
+
+        def load_rows(src, name):
+            held = keep.tile([P, PACK], F32, name=name)
+            nc.gpsimd.dma_start(held[:], src.rearrange("(p t) o -> p (t o)", t=PACK))
+            return held
+
+        gn_c = load_rows(gn, "gn_c")
+        sl_c = load_rows(sl, "sl_c")
+        th_c = load_rows(th, "th_c")
+
+        key_bytes = keep.tile([P, H], U8, name="key_bytes")
+        nc.vector.tensor_copy(key_bytes[:], d_bytes[:].indirect(k1_l[:]))
+        key_scales = keep.tile([P, H], U8, name="key_scales", align_bytes=64)
+        nc.vector.tensor_copy(
+            key_scales[:].rearrange("p (t m) -> p m t", t=PACK), key_bytes[:].rearrange("p (m t) -> p m t", t=PACK)
+        )
+        for e in range(2):
+            nc.scalar.dma_start(key_scales[2 + e : P : 32, :].bitcast(I32), key_scales[16 + e : P : 32, :].bitcast(I32))
+
+
+        key_words = keep.tile([P, H], U32, name="key_words", tag="slot_d")
+        nc.vector.tensor_copy(key_words[:], d_tab[:].indirect(k1_l[:]))
+        key_codes = keep.tile([P, H], I32, name="key_codes", align_bytes=64)
+        nc.vector.tensor_copy(
+            key_codes[:].rearrange("p (t m) -> p m t", t=PACK),
+            key_words[:].bitcast(I32).rearrange("p (m t) -> p m t", t=PACK),
+        )
+        w2_raw = keep.tile([P, PACK, N], F32, name="w2_raw", tag="slot_b")
+        nc.sync.dma_start(w2_raw[:], w2.rearrange("(p j) c -> p j c", j=PACK))
+        w1_hi = keep.tile([P, PACK, half_n], F32, name="w1_hi", tag="slot_d")
+        nc.sync.dma_start(w1_hi[:], w1_rows[:, :, half_n:])
+
+        xq_scales = keep.tile([P, S], U8, name="xq_scales", align_bytes=64)
+        nc.vector.tensor_copy(xq_scales[:], x_bytes[:].indirect(offs_l[:]))
+        xq_codes = keep.tile([P, S], U32, name="xq_codes", align_bytes=64)
+        nc.vector.tensor_copy(xq_codes[:], x_tab[:].indirect(offs_l[:]))
+
+        s_ps = [psum.tile([P, S], F32, name="s_ps%d" % t) for t in range(PACK)]
+        for t in range(PACK):
+            cols = slice(P * t, P * (t + 1))
+            nc.tensor.matmul_mx(
+                out=s_ps[t][:],
+                lhsT=key_codes[:, cols].bitcast(FP8X4),
+                lhsT_scale=key_scales[:, cols],
+                rhs=xq_codes[:].bitcast(FP8X4),
+                rhs_scale=xq_scales[:],
+                start=True,
+                stop=True,
+            )
+
+        x2_codes = keep.tile([P, S], U32, name="x2_codes", align_bytes=64)
+        nc.vector.tensor_copy(x2_codes[:], x_tab[:].indirect(two_l[:]))
+        x2_scales = keep.tile([P, S], U8, name="x2_scales", tag="slot_c", align_bytes=64)
+        nc.vector.tensor_copy(x2_scales[:], x_bytes[:].indirect(two_l[:]))
+
+        slth = keep.tile([P, PACK], F32, name="slth")
+        nc.gpsimd.tensor_tensor(slth[:], sl_c[:], th_c[:], ALU.mult)
+        bias_c = keep.tile([P, PACK], F32, name="bias_c")
+        nc.gpsimd.tensor_scalar(bias_c[:], slth[:], -1.0, 0.0, ALU.mult, ALU.add)
+
+        def deal(copy, grouped, raw, m0, m1):
+            copy(
+                grouped[:].rearrange("p (t m j) -> p m j t", t=PACK, j=PACK)[:, m0:m1],
+                raw[:].rearrange("p j (m t) -> p m j t", t=PACK),
+            )
+
+        w2_g = keep.tile([P, PACK * N], BF16, name="w2_g", align_bytes=64)
+        w1_g = keep.tile([P, PACK * N], BF16, name="w1_g", align_bytes=64)
+        deal(nc.scalar.copy, w1_g, w1_lo, 0, P // 2)
+
+        s_sb = []
+        for t in range(PACK):
+            s_t = keep.tile([P, S], F32, name="s_sb%d" % t)
+            nc.scalar.activation(s_t[:], s_ps[t][:], ACT.Copy, scale=0.0625)
+            pa = keep.tile([P, W], F32, name="pa%d" % t, tag="pa%d" % t)
+            nc.scalar.activation(pa[:], s_t[:].indirect(n1_l[:]), ACT.Copy)
+            pb = keep.tile([P, W], F32, name="pb%d" % t, tag="pb%d" % t)
+            nc.scalar.activation(pb[:], s_t[:].indirect(n2_l[:]), ACT.Copy)
+            ra = keep.tile([P, W], F32, name="ra%d" % t)
+            nc.vector.tensor_tensor(ra[:], pa[:], pb[:], ALU.max)
+            nc.vector.tensor_copy(s_t[:].indirect(n1_l[:]), ra[:])
+            s_sb.append(s_t)
+
+        def quantise(grouped, name):
+            width = grouped.shape[1] // PACK
+            codes = keep.tile([P, width], U32, name=name + "_codes", align_bytes=64)
+            scales = keep.tile([P, width], U8, name=name + "_scales", align_bytes=64)
+            nc.vector.quantize_mx(out=codes[:].bitcast(FP8X4), scales=scales[:], in_=grouped[:])
+            return codes, scales
+
+        deal(nc.scalar.copy, w1_g, w1_hi, P // 2, P)
+        deal(nc.vector.tensor_copy, w2_g, w2_raw, 0, P)
+        w2_codes, w2_scales = quantise(w2_g, "w2")
+        w1_codes, w1_scales = quantise(w1_g, "w1")
+
+        half = S // 2
+        z_pairs = [keep.tile([P, PACK * half], BF16, name="z_pairs%d" % a, tag=("pa2", "pb2")[a]) for a in range(2)]
+        for t in range(PACK):
+            for a in range(2):
+                nc.scalar.activation(
+                    z_pairs[a][:].rearrange("p (u c e) -> p u e c", u=2, e=2)[:, t // 2, t % 2, :],
+                    s_sb[t][:, a * half : (a + 1) * half],
+                    ACT.Copy,
+                    scale=gn_c[:, t : t + 1],
+                )
+        z_g = [keep.tile([P, PACK * half], BF16, name="z_g%d" % a, align_bytes=64) for a in range(2)]
+        for a in range(2):
+            nc.vector.tensor_copy(
+                z_g[a][:].bitcast(I32).rearrange("p (c u) -> p c u", u=2),
+                z_pairs[a][:].bitcast(I32).rearrange("p (u c) -> p c u", u=2),
+            )
+        z_mx = [quantise(z_g[a], "z%d" % a) for a in range(2)]
+
+        h_ps = [psum.tile([P, S], F32, name="h_ps%d" % t) for t in range(PACK)]
+        for t in range(PACK):
+            cols = slice(P * t, P * (t + 1))
+            nc.tensor.matmul_mx(
+                out=h_ps[t][:],
+                lhsT=w2_codes[:, cols].bitcast(FP8X4),
+                lhsT_scale=w2_scales[:, cols],
+                rhs=x2_codes[:].bitcast(FP8X4),
+                rhs_scale=x2_scales[:],
+                start=True,
+                stop=False,
+            )
+        for a in range(2):
+            for t in range(PACK):
+                cols = slice(P * t, P * (t + 1))
+                nc.tensor.matmul_mx(
+                    out=h_ps[t][:, a * half : (a + 1) * half],
+                    lhsT=w1_codes[:, cols].bitcast(FP8X4),
+                    lhsT_scale=w1_scales[:, cols],
+                    rhs=z_mx[a][0][:].bitcast(FP8X4),
+                    rhs_scale=z_mx[a][1][:],
+                    start=False,
+                    stop=(a == 1),
+                )
+
+        out_rows = out.rearrange("(p t) n -> t p n", t=PACK)
+        h_sb = [keep.tile([P, S], F32, name="h_sb%d" % t) for t in range(PACK)]
+        far = [keep.tile([P, S], F32, name="far%d" % t) for t in range(PACK)]
+        st = [keep.tile([P, S], F32, name="st%d" % t) for t in range(PACK)]
+        for t in range(PACK):
+            nc.scalar.copy(h_sb[t][:], h_ps[t][:])
+            for u in range(2):
+                window = h_sb[t][:].indirect(n3_l[:, u * half // 16 : (u + 1) * half // 16])
+                if (t, u) == (2, 0):
+                    nc.scalar.activation(far[t][:, u * half : (u + 1) * half], window, ACT.Copy)
+                else:
+                    nc.vector.tensor_copy(far[t][:, u * half : (u + 1) * half], window)
+            nc.vector.tensor_tensor(st[t][:], h_sb[t][:], far[t][:], ALU.max)
+        for t in range(PACK):
+            sg = keep.tile([P, S], F32, name="sg%d" % t)
+            for u in range(2):
+                nc.scalar.activation(
+                    sg[:, u * half : (u + 1) * half],
+                    st[t][:].indirect(n4_l[:, u * half // 16 : (u + 1) * half // 16]),
+                    ACT.Sigmoid,
+                    scale=sl_c[:, t : t + 1],
+                    bias=bias_c[:, t : t + 1],
+                )
+            res = keep.tile([P, S], F32, name="res%d" % t)
+            nc.vector.tensor_tensor(res[:], st[t][:], sg[:], ALU.mult)
+            nc.sync.dma_start(out_rows[t], res[:])

@@ -17,6 +17,7 @@ ACT = mybir.ActivationFunctionType
 
 P = 128
 PACK = 4
+DEAL_STEP = 32
 
 
 def tile_picked_kmixfillehh_none_p_kernel(
@@ -33,7 +34,7 @@ def tile_picked_kmixfillehh_none_p_kernel(
             nc.sync.dma_start(held[:], src)
             return held
 
-        d_bytes = keep.tile([P, G], U8, name="d_bytes")
+        d_bytes = keep.tile([P, G], U8, name="d_bytes", tag="slot_e")
         x_bytes = keep.tile([P, T], U8, name="x_bytes")
         for table in (d_bytes, x_bytes):
             nc.vector.memset(table[:, : T // 2].bitcast(I32), 0)
@@ -51,25 +52,12 @@ def tile_picked_kmixfillehh_none_p_kernel(
             nc.sync.dma_start(x_bytes[32 * q : 32 * q + 4, :].bitcast(I32), x_scales[0, 4 * q : 4 * q + 4, :].bitcast(I32))
         x_tab = keep.tile([P, T], U32, name="x_tab", tag="slot_c", align_bytes=64)
         nc.sync.dma_start(x_tab[:].bitcast(I32), x_words[0].rearrange("p n t -> p (n t)").bitcast(I32))
-        half_n = N // 2
-        w1_rows = w1.rearrange("(p j) c -> p j c", j=PACK)
-        w1_lo = keep.tile([P, PACK, half_n], F32, name="w1_lo")
-        nc.sync.dma_start(w1_lo[:], w1_rows[:, :, :half_n])
         n1_l = load_list(n1, "n1_l")
         n2_l = load_list(n2, "n2_l")
         n3_l = load_list(n3, "n3_l")
         n4_l = load_list(n4, "n4_l")
 
-        def load_rows(src, name):
-            held = keep.tile([P, PACK], F32, name=name)
-            nc.gpsimd.dma_start(held[:], src.rearrange("(p t) o -> p (t o)", t=PACK))
-            return held
-
-        gn_c = load_rows(gn, "gn_c")
-        sl_c = load_rows(sl, "sl_c")
-        th_c = load_rows(th, "th_c")
-
-        key_bytes = keep.tile([P, H], U8, name="key_bytes")
+        key_bytes = keep.tile([P, H], U8, name="key_bytes", tag="slot_a")
         nc.vector.tensor_copy(key_bytes[:], d_bytes[:].indirect(k1_l[:]))
         key_scales = keep.tile([P, H], U8, name="key_scales", align_bytes=64)
         nc.vector.tensor_copy(
@@ -79,17 +67,23 @@ def tile_picked_kmixfillehh_none_p_kernel(
             nc.scalar.dma_start(key_scales[2 + e : P : 32, :].bitcast(I32), key_scales[16 + e : P : 32, :].bitcast(I32))
 
 
-        key_words = keep.tile([P, H], U32, name="key_words", tag="slot_d")
+        rowwise = keep.tile([P, 3, 8], F32, name="rowwise", tag="slot_e")
+        for i, src in enumerate((sl, th, gn)):
+            nc.gpsimd.dma_start(rowwise[:, i, :PACK], src.rearrange("(p t) o -> p (t o)", t=PACK))
+        sl_c, th_c, gn_c = (rowwise[:, i, :PACK] for i in range(3))
+
+        w2_raw = keep.tile([P, PACK, N], F32, name="w2_raw", tag="slot_a")
+        nc.sync.dma_start(w2_raw[:], w2.rearrange("(p j) c -> p j c", j=PACK))
+
+        key_words = keep.tile([P, H], U32, name="key_words")
         nc.vector.tensor_copy(key_words[:], d_tab[:].indirect(k1_l[:]))
         key_codes = keep.tile([P, H], I32, name="key_codes", align_bytes=64)
         nc.vector.tensor_copy(
             key_codes[:].rearrange("p (t m) -> p m t", t=PACK),
             key_words[:].bitcast(I32).rearrange("p (m t) -> p m t", t=PACK),
         )
-        w2_raw = keep.tile([P, PACK, N], F32, name="w2_raw", tag="slot_b")
-        nc.sync.dma_start(w2_raw[:], w2.rearrange("(p j) c -> p j c", j=PACK))
-        w1_hi = keep.tile([P, PACK, half_n], F32, name="w1_hi", tag="slot_d")
-        nc.sync.dma_start(w1_hi[:], w1_rows[:, :, half_n:])
+        w1_raw = keep.tile([P, PACK, N], F32, name="w1_raw", tag="slot_b")
+        nc.sync.dma_start(w1_raw[:], w1.rearrange("(p j) c -> p j c", j=PACK))
 
         xq_scales = keep.tile([P, S], U8, name="xq_scales", align_bytes=64)
         nc.vector.tensor_copy(xq_scales[:], x_bytes[:].indirect(offs_l[:]))
@@ -115,32 +109,35 @@ def tile_picked_kmixfillehh_none_p_kernel(
         nc.vector.tensor_copy(x2_scales[:], x_bytes[:].indirect(two_l[:]))
 
         slth = keep.tile([P, PACK], F32, name="slth")
-        nc.gpsimd.tensor_tensor(slth[:], sl_c[:], th_c[:], ALU.mult)
+        nc.gpsimd.tensor_tensor(slth[:], sl_c, th_c, ALU.mult)
         bias_c = keep.tile([P, PACK], F32, name="bias_c")
         nc.gpsimd.tensor_scalar(bias_c[:], slth[:], -1.0, 0.0, ALU.mult, ALU.add)
 
-        def deal(copy, grouped, raw, m0, m1):
-            copy(
-                grouped[:].rearrange("p (t m j) -> p m j t", t=PACK, j=PACK)[:, m0:m1],
-                raw[:].rearrange("p j (m t) -> p m j t", t=PACK),
-            )
+        def deal(raw, name):
+            grouped = keep.tile([P, PACK * N], BF16, name=name, align_bytes=64)
+            dealt = grouped[:].rearrange("p (t m j) -> p m t j", t=PACK, j=PACK)
+            natural = raw[:].rearrange("p j (m t) -> p m t j", t=PACK)
+            for m0 in range(0, P, DEAL_STEP):
+                nc.gpsimd.tensor_scalar(
+                    dealt[:, m0 : m0 + DEAL_STEP], natural[:, m0 : m0 + DEAL_STEP], 1.0, 0.0, ALU.mult, ALU.add
+                )
+            return grouped
 
-        w2_g = keep.tile([P, PACK * N], BF16, name="w2_g", align_bytes=64)
-        w1_g = keep.tile([P, PACK * N], BF16, name="w1_g", align_bytes=64)
-        deal(nc.scalar.copy, w1_g, w1_lo, 0, P // 2)
+        w2_g = deal(w2_raw, "w2_g")
+        w1_g = deal(w1_raw, "w1_g")
 
-        s_sb = []
+        s_sb = [keep.tile([P, S], F32, name="s_sb%d" % t, tag="s_sb%d" % t) for t in range(PACK)]
+        nc.scalar.activation(s_sb[0][:], s_ps[0][:], ACT.Copy, scale=0.0625)
         for t in range(PACK):
-            s_t = keep.tile([P, S], F32, name="s_sb%d" % t)
-            nc.scalar.activation(s_t[:], s_ps[t][:], ACT.Copy, scale=0.0625)
+            for ahead in {0: (), 1: (1, 2), 2: (3,), 3: ()}[t]:
+                nc.scalar.activation(s_sb[ahead][:], s_ps[ahead][:], ACT.Copy, scale=0.0625)
             pa = keep.tile([P, W], F32, name="pa%d" % t, tag="pa%d" % t)
-            nc.scalar.activation(pa[:], s_t[:].indirect(n1_l[:]), ACT.Copy)
+            nc.scalar.activation(pa[:], s_sb[t][:].indirect(n1_l[:]), ACT.Copy)
             pb = keep.tile([P, W], F32, name="pb%d" % t, tag="pb%d" % t)
-            nc.scalar.activation(pb[:], s_t[:].indirect(n2_l[:]), ACT.Copy)
+            nc.scalar.activation(pb[:], s_sb[t][:].indirect(n2_l[:]), ACT.Copy)
             ra = keep.tile([P, W], F32, name="ra%d" % t)
             nc.vector.tensor_tensor(ra[:], pa[:], pb[:], ALU.max)
-            nc.vector.tensor_copy(s_t[:].indirect(n1_l[:]), ra[:])
-            s_sb.append(s_t)
+            nc.vector.tensor_copy(s_sb[t][:].indirect(n1_l[:]), ra[:])
 
         def quantise(grouped, name):
             width = grouped.shape[1] // PACK
@@ -149,8 +146,6 @@ def tile_picked_kmixfillehh_none_p_kernel(
             nc.vector.quantize_mx(out=codes[:].bitcast(FP8X4), scales=scales[:], in_=grouped[:])
             return codes, scales
 
-        deal(nc.scalar.copy, w1_g, w1_hi, P // 2, P)
-        deal(nc.vector.tensor_copy, w2_g, w2_raw, 0, P)
         w2_codes, w2_scales = quantise(w2_g, "w2")
         w1_codes, w1_scales = quantise(w1_g, "w1")
 
@@ -184,8 +179,8 @@ def tile_picked_kmixfillehh_none_p_kernel(
                 start=True,
                 stop=False,
             )
-        for a in range(2):
-            for t in range(PACK):
+        for t in range(PACK):
+            for a in range(2):
                 cols = slice(P * t, P * (t + 1))
                 nc.tensor.matmul_mx(
                     out=h_ps[t][:, a * half : (a + 1) * half],
@@ -221,5 +216,8 @@ def tile_picked_kmixfillehh_none_p_kernel(
                     bias=bias_c[:, t : t + 1],
                 )
             res = keep.tile([P, S], F32, name="res%d" % t)
-            nc.vector.tensor_tensor(res[:], st[t][:], sg[:], ALU.mult)
-            nc.sync.dma_start(out_rows[t], res[:])
+            step = half if t == PACK - 1 else S
+            for c0 in range(0, S, step):
+                cols = slice(c0, c0 + step)
+                nc.vector.tensor_tensor(res[:, cols], st[t][:, cols], sg[:, cols], ALU.mult)
+                nc.sync.dma_start(out_rows[t][:, cols], res[:, cols])

from contextlib import ExitStack

import concourse.mybir as mybir

K, T, S, N, G, H, W = 512, 2048, 512, 512, 2048, 512, 256
FLOPS = 2 * K * H * S + 2 * H * N * S + 2 * K * N * S

F32 = mybir.dt.float32
BF16 = mybir.dt.bfloat16
I32 = mybir.dt.int32
U32 = mybir.dt.uint32
U16 = mybir.dt.uint16
U8 = mybir.dt.uint8
FP8X4 = mybir.dt.float8_e4m3fn_x4
ALU = mybir.AluOpType
ACT = mybir.ActivationFunctionType

P = 128
PACK = 4
DEAL_STEP = 32


def tile_picked_kmixfillehh_none_p_kernel(
    tc, x_words, x_scales, d_words, d_scales, gn, w1, w2, sl, th, offs, k1, n1, n2, two, n3, n4, out
):
    nc = tc.nc
    with ExitStack() as ctx:
        lists = ctx.enter_context(tc.tile_pool(name="lists", bufs=1))
        keep = ctx.enter_context(tc.tile_pool(name="keep", bufs=1))
        psum = ctx.enter_context(tc.psum_pool(name="psum", bufs=1))

        def load_list(src, name):
            held = lists.tile(list(src.shape), U16, name=name)
            nc.sync.dma_start(held[:], src)
            return held

        d_bytes = keep.tile([P, G], U8, name="d_bytes", tag="slot_e")
        x_bytes = keep.tile([P, T], U8, name="x_bytes")
        for table in (d_bytes, x_bytes):
            nc.vector.memset(table[:, : T // 2].bitcast(I32), 0)
            nc.gpsimd.memset(table[:, T // 2 :].bitcast(I32), 0)

        k1_l = load_list(k1, "k1_l")
        d_rows = d_scales[0].rearrange("(g e) c -> e g c", e=2)
        for e in range(2):
            nc.sync.dma_start(d_bytes[e:P:16, :].bitcast(I32), d_rows[e].bitcast(I32))
        offs_l = load_list(offs, "offs_l")
        two_l = load_list(two, "two_l")
        d_tab = keep.tile([P, G], U32, name="d_tab", tag="slot_b")
        nc.sync.dma_start(d_tab[:].bitcast(I32), d_words[0].rearrange("p n t -> p (n t)").bitcast(I32))
        for q in range(4):
            nc.sync.dma_start(x_bytes[32 * q : 32 * q + 4, :].bitcast(I32), x_scales[0, 4 * q : 4 * q + 4, :].bitcast(I32))
        x_tab = keep.tile([P, T], U32, name="x_tab", tag="slot_c", align_bytes=64)
        nc.sync.dma_start(x_tab[:].bitcast(I32), x_words[0].rearrange("p n t -> p (n t)").bitcast(I32))
        n1_l = load_list(n1, "n1_l")
        n2_l = load_list(n2, "n2_l")
        n3_l = load_list(n3, "n3_l")
        n4_l = load_list(n4, "n4_l")

        key_bytes = keep.tile([P, H], U8, name="key_bytes", tag="slot_a")
        nc.vector.tensor_copy(key_bytes[:], d_bytes[:].indirect(k1_l[:]))
        key_scales = keep.tile([P, H], U8, name="key_scales", align_bytes=64)
        nc.vector.tensor_copy(
            key_scales[:].rearrange("p (t m) -> p m t", t=PACK), key_bytes[:].rearrange("p (m t) -> p m t", t=PACK)
        )
        for e in range(2):
            nc.scalar.dma_start(key_scales[2 + e : P : 32, :].bitcast(I32), key_scales[16 + e : P : 32, :].bitcast(I32))


        rowwise = keep.tile([P, 3, 8], F32, name="rowwise", tag="slot_e")
        for i, src in enumerate((sl, th, gn)):
            nc.gpsimd.dma_start(rowwise[:, i, :PACK], src.rearrange("(p t) o -> p (t o)", t=PACK))
        sl_c, th_c, gn_c = (rowwise[:, i, :PACK] for i in range(3))

        w2_raw = keep.tile([P, PACK, N], F32, name="w2_raw", tag="slot_a")
        nc.sync.dma_start(w2_raw[:], w2.rearrange("(p j) c -> p j c", j=PACK))

        key_words = keep.tile([P, H], U32, name="key_words")
        nc.vector.tensor_copy(key_words[:], d_tab[:].indirect(k1_l[:]))
        key_codes = keep.tile([P, H], I32, name="key_codes", align_bytes=64)
        nc.vector.tensor_copy(
            key_codes[:].rearrange("p (t m) -> p m t", t=PACK),
            key_words[:].bitcast(I32).rearrange("p (m t) -> p m t", t=PACK),
        )
        w1_raw = keep.tile([P, PACK, N], F32, name="w1_raw", tag="slot_b")
        nc.sync.dma_start(w1_raw[:], w1.rearrange("(p j) c -> p j c", j=PACK))

        xq_scales = keep.tile([P, S], U8, name="xq_scales", align_bytes=64)
        nc.vector.tensor_copy(xq_scales[:], x_bytes[:].indirect(offs_l[:]))
        xq_codes = keep.tile([P, S], U32, name="xq_codes", align_bytes=64)
        nc.vector.tensor_copy(xq_codes[:], x_tab[:].indirect(offs_l[:]))

        s_ps = [psum.tile([P, S], F32, name="s_ps%d" % t) for t in range(PACK)]
        for t in range(PACK):
            cols = slice(P * t, P * (t + 1))
            nc.tensor.matmul_mx(
                out=s_ps[t][:],
                lhsT=key_codes[:, cols].bitcast(FP8X4),
                lhsT_scale=key_scales[:, cols],
                rhs=xq_codes[:].bitcast(FP8X4),
                rhs_scale=xq_scales[:],
                start=True,
                stop=True,
            )

        x2_codes = keep.tile([P, S], U32, name="x2_codes", align_bytes=64)
        nc.vector.tensor_copy(x2_codes[:], x_tab[:].indirect(two_l[:]))
        x2_scales = keep.tile([P, S], U8, name="x2_scales", tag="slot_c", align_bytes=64)
        nc.vector.tensor_copy(x2_scales[:], x_bytes[:].indirect(two_l[:]))

        slth = keep.tile([P, PACK], F32, name="slth")
        nc.gpsimd.tensor_tensor(slth[:], sl_c, th_c, ALU.mult)
        bias_c = keep.tile([P, PACK], F32, name="bias_c")
        nc.gpsimd.tensor_scalar(bias_c[:], slth[:], -1.0, 0.0, ALU.mult, ALU.add)

        def deal(raw, name):
            grouped = keep.tile([P, PACK * N], BF16, name=name, align_bytes=64)
            dealt = grouped[:].rearrange("p (t m j) -> p m t j", t=PACK, j=PACK)
            natural = raw[:].rearrange("p j (m t) -> p m t j", t=PACK)
            for m0 in range(0, P, DEAL_STEP):
                nc.gpsimd.tensor_scalar(
                    dealt[:, m0 : m0 + DEAL_STEP], natural[:, m0 : m0 + DEAL_STEP], 1.0, 0.0, ALU.mult, ALU.add
                )
            return grouped

        w2_g = deal(w2_raw, "w2_g")
        w1_g = deal(w1_raw, "w1_g")

        s_sb = [keep.tile([P, S], F32, name="s_sb%d" % t, tag="s_sb%d" % t) for t in range(PACK)]
        nc.scalar.activation(s_sb[0][:], s_ps[0][:], ACT.Copy, scale=0.0625)
        for t in range(PACK):
            for ahead in {0: (), 1: (1, 2), 2: (3,), 3: ()}[t]:
                nc.scalar.activation(s_sb[ahead][:], s_ps[ahead][:], ACT.Copy, scale=0.0625)
            pa = keep.tile([P, W], F32, name="pa%d" % t, tag="pa%d" % t)
            nc.scalar.activation(pa[:], s_sb[t][:].indirect(n1_l[:]), ACT.Copy)
            pb = keep.tile([P, W], F32, name="pb%d" % t, tag="pb%d" % t)
            nc.scalar.activation(pb[:], s_sb[t][:].indirect(n2_l[:]), ACT.Copy)
            ra = keep.tile([P, W], F32, name="ra%d" % t)
            nc.vector.tensor_tensor(ra[:], pa[:], pb[:], ALU.max)
            nc.vector.tensor_copy(s_sb[t][:].indirect(n1_l[:]), ra[:])

        def quantise(grouped, name):
            width = grouped.shape[1] // PACK
            codes = keep.tile([P, width], U32, name=name + "_codes", align_bytes=64)
            scales = keep.tile([P, width], U8, name=name + "_scales", align_bytes=64)
            nc.vector.quantize_mx(out=codes[:].bitcast(FP8X4), scales=scales[:], in_=grouped[:])
            return codes, scales

        w2_codes, w2_scales = quantise(w2_g, "w2")
        w1_codes, w1_scales = quantise(w1_g, "w1")

        half = S // 2
        z_pairs = [keep.tile([P, PACK * half], BF16, name="z_pairs%d" % a, tag=("pa2", "pb2")[a]) for a in range(2)]
        for t in range(PACK):
            for a in range(2):
                nc.scalar.activation(
                    z_pairs[a][:].rearrange("p (u c e) -> p u e c", u=2, e=2)[:, t // 2, t % 2, :],
                    s_sb[t][:, a * half : (a + 1) * half],
                    ACT.Copy,
                    scale=gn_c[:, t : t + 1],
                )
        z_g = [keep.tile([P, PACK * half], BF16, name="z_g%d" % a, align_bytes=64) for a in range(2)]
        for a in range(2):
            nc.vector.tensor_copy(
                z_g[a][:].bitcast(I32).rearrange("p (c u) -> p c u", u=2),
                z_pairs[a][:].bitcast(I32).rearrange("p (u c) -> p c u", u=2),
            )
        z_mx = [quantise(z_g[a], "z%d" % a) for a in range(2)]

        h_ps = [psum.tile([P, S], F32, name="h_ps%d" % t) for t in range(PACK)]
        for t in range(PACK):
            cols = slice(P * t, P * (t + 1))
            nc.tensor.matmul_mx(
                out=h_ps[t][:],
                lhsT=w2_codes[:, cols].bitcast(FP8X4),
                lhsT_scale=w2_scales[:, cols],
                rhs=x2_codes[:].bitcast(FP8X4),
                rhs_scale=x2_scales[:],
                start=True,
                stop=False,
            )
        for t in range(PACK):
            for a in range(2):
                cols = slice(P * t, P * (t + 1))
                nc.tensor.matmul_mx(
                    out=h_ps[t][:, a * half : (a + 1) * half],
                    lhsT=w1_codes[:, cols].bitcast(FP8X4),
                    lhsT_scale=w1_scales[:, cols],
                    rhs=z_mx[a][0][:].bitcast(FP8X4),
                    rhs_scale=z_mx[a][1][:],
                    start=False,
                    stop=(a == 1),
                )

        out_rows = out.rearrange("(p t) n -> t p n", t=PACK)
        h_sb = [keep.tile([P, S], F32, name="h_sb%d" % t) for t in range(PACK)]
        far = [keep.tile([P, S], F32, name="far%d" % t) for t in range(PACK)]
        st = [keep.tile([P, S], F32, name="st%d" % t) for t in range(PACK)]
        for t in range(PACK):
            nc.scalar.copy(h_sb[t][:], h_ps[t][:])
            for u in range(2):
                window = h_sb[t][:].indirect(n3_l[:, u * half // 16 : (u + 1) * half // 16])
                if (t, u) == (2, 0):
                    nc.scalar.activation(far[t][:, u * half : (u + 1) * half], window, ACT.Copy)
                else:
                    nc.vector.tensor_copy(far[t][:, u * half : (u + 1) * half], window)
            nc.vector.tensor_tensor(st[t][:], h_sb[t][:], far[t][:], ALU.max)
        for t in range(PACK):
            sg = keep.tile([P, S], F32, name="sg%d" % t)
            for u in range(2):
                nc.scalar.activation(
                    sg[:, u * half : (u + 1) * half],
                    st[t][:].indirect(n4_l[:, u * half // 16 : (u + 1) * half // 16]),
                    ACT.Sigmoid,
                    scale=sl_c[:, t : t + 1],
                    bias=bias_c[:, t : t + 1],
                )
            res = keep.tile([P, S], F32, name="res%d" % t)
            step = half if t == PACK - 1 else S
            for c0 in range(0, S, step):
                cols = slice(c0, c0 + step)
                nc.vector.tensor_tensor(res[:, cols], st[t][:, cols], sg[:, cols], ALU.mult)
                nc.sync.dma_start(out_rows[t][:, cols], res[:, cols])
